import numpy as np
import ml_dtypes


def mxq(x, axis, fmt="e4m3"):
    dtype, down = {"e4m3": (ml_dtypes.float8_e4m3fn, 7), "e5m2": (ml_dtypes.float8_e5m2, 14)}[fmt]
    v = np.moveaxis(np.asarray(x, np.float32).astype(ml_dtypes.bfloat16).astype(np.float64), axis, -1)
    blocks = v.reshape(v.shape[:-1] + (-1, 32))
    amax = np.abs(blocks).max(-1, keepdims=True)
    byte = np.maximum(np.where(amax > 0, np.frexp(amax)[1] - 1 + 127, 0) - down, 1)
    scale = np.exp2(byte - 127.0)
    codes = (blocks / scale).astype(np.float32).astype(dtype).astype(np.float64)
    return np.moveaxis((codes * scale).reshape(v.shape), -1, axis)


WIDE = False


def mx_kscale(k):
    if not WIDE:
        return np.ones(k)
    levels = np.array([10, -10, 5, -5, 0])
    if k % 512:
        return np.exp2(np.random.permutation(np.resize(levels, k // 32))).repeat(32)
    a = np.empty((k // 512, 16))
    for p in range(k // 512):
        a[p, :8] = np.random.permutation(np.resize(levels, 8))
        for g in range(8):
            far = levels[np.abs(levels - a[p, g]) >= 10]
            a[p, g + 8] = far[np.random.randint(len(far))]
    return np.exp2(a.ravel()).repeat(32)


def f64(x):
    return np.asarray(x).astype(np.float64)


def striped(idx):
    return np.tile(idx.reshape(-1, 16).T, (8, 1)).astype(np.uint16)


def unstriped(offs):
    return offs[:16].T.reshape(-1).astype(np.int64)


def pack_weight(w):
    k, n = w.shape
    w = f64(np.asarray(w, np.float32).astype(ml_dtypes.bfloat16)).reshape(k // 32, 32, n)
    amax = np.abs(w).max(1)
    byte = np.clip(np.where(amax > 0, np.frexp(amax)[1] - 1 + 127 - 7, 1), 1, 254)
    scaled = (w * np.exp2(127.0 - byte)[:, None, :]).reshape(k, n).astype(np.float32)
    words = np.ascontiguousarray(scaled.reshape(k // 512, 128, 4, n).transpose(0, 1, 3, 2)).astype(ml_dtypes.float8_e4m3fn).view(np.uint8)
    return words, np.ascontiguousarray(byte.astype(np.uint8).reshape(k // 512, 16, n))


def unpack_weight(words, scales):
    g, p, n, _ = words.shape
    vals = np.ascontiguousarray(words).view(ml_dtypes.float8_e4m3fn).astype(np.float64) * np.repeat(np.exp2(scales.astype(np.float64) - 127.0), 8, axis=1)[..., None]
    return vals.transpose(0, 1, 3, 2).reshape(g * 512, n)


K, T, S, N = 512, 1024, 512, 128
P = 2 ** 7


def setup_inputs():
    n = np.random.standard_normal
    s = mx_kscale(K)[:, None]
    packed_xT = pack_weight(n((K, T)) * s)
    return {
        "x_words": packed_xT[0],
        "x_scales": packed_xT[1],
        "w1": (n((K, N)) / np.sqrt(K) / s).astype(np.float32),
        "flow": (np.random.uniform(0.2, 2.0, (N, S))).astype(np.float32),
        "infl": (np.random.uniform(0.2, 2.0, (N, S))).astype(np.float32),
        "cou": (np.tile(np.random.uniform(0.2, 0.8, S), (P, 1))).astype(np.float32),
        "bank": (np.random.uniform(0.2, 0.8, (N, 1))).astype(np.float32),
        "offs": striped(np.random.permutation(T)[:S]),
        "tra": striped(np.random.permutation(S)),
        "trb": striped(np.random.permutation(S)),
    }


def reference(x_words, x_scales, w1, flow, infl, cou, bank, offs, tra, trb):
    xq = unpack_weight(x_words, x_scales)[:, unstriped(offs)]
    y = mxq(f64(w1), 0, "e4m3").T @ xq
    lat = np.log(np.exp(y) + 1.0)
    oa = (f64(cou)[:1] * lat + f64(cou)[:1] * f64(infl) + (-1.0 * (0.5 * f64(cou)[:1]) + 1.0) * f64(flow)) / (1.5 * f64(cou)[:1] + 1.0)
    ib = 0.6 * (oa[:, unstriped(tra)] + oa[:, unstriped(trb)]) + 0.3 * lat
    return np.exp(0.6 * (np.log((f64(cou)[:1] * ib + f64(cou)[:1] * lat + (-1.0 * (0.5 * f64(cou)[:1]) + 1.0) * oa) / (1.5 * f64(cou)[:1] + 1.0) + 0.1))) - (f64(bank) * oa)

@@ -1,0 +1,168 @@
+from contextlib import ExitStack
+
+import concourse.mybir as mybir
+from concourse.masks import make_identity
+
+K, T, S, N = 512, 1024, 512, 128
+FLOPS = 2 * K * N * S
+
+F32 = mybir.dt.float32
+BF16 = mybir.dt.bfloat16
+I32 = mybir.dt.int32
+U32 = mybir.dt.uint32
+U16 = mybir.dt.uint16
+U8 = mybir.dt.uint8
+FP8X4 = mybir.dt.float8_e4m3fn_x4
+ALU = mybir.AluOpType
+ACT = mybir.ActivationFunctionType
+
+P = 128
+PACK = 4
+CHUNKS = S // P
+HALF = S // 2
+SIGMA = 0.6 / 2.3
+GUARD = 2.0 ** -40
+
+
+def tile_picked_ymuskr_stage_p_kernel(tc, x_words, x_scales, w1, flow, infl, cou, bank, offs, tra, trb, out):
+    nc = tc.nc
+    with ExitStack() as ctx:
+        lists = ctx.enter_context(tc.tile_pool(name="lists", bufs=1))
+        sb = ctx.enter_context(tc.tile_pool(name="sb", bufs=1))
+        ps = ctx.enter_context(tc.psum_pool(name="ps", bufs=1))
+
+        def chunk(t):
+            return slice(t * P, (t + 1) * P)
+
+        def half(h):
+            return slice(h * HALF, (h + 1) * HALF)
+
+        def entries(cols):
+            return slice(cols.start // 16, cols.stop // 16)
+
+        offs_sb = lists.tile([P, S // 16], U16, name="offs_sb")
+        tra_sb = lists.tile([P, S // 16], U16, name="tra_sb")
+        trb_sb = lists.tile([P, S // 16], U16, name="trb_sb")
+
+        scale_table = sb.tile([P, T], U8, name="scale_table", align_bytes=64)
+        word_table = sb.tile([P, T], U32, name="word_table", align_bytes=64)
+        w_raw = sb.tile([P, PACK, N], F32, name="w_raw")
+        c_col = sb.tile([P, CHUNKS], F32, name="c_col")
+        flow_sb = sb.tile([P, S], F32, name="flow_sb")
+        infl_sb = sb.tile([P, S], F32, name="infl_sb")
+        bank_sb = sb.tile([P, 1], F32, name="bank_sb")
+
+        nc.vector.memset(scale_table[:].bitcast(I32), 0)
+        nc.sync.dma_start(offs_sb[:], offs)
+        with nc.allow_non_contiguous_dma(reason="one routing number a partition and chunk"):
+            nc.sync.dma_start(c_col[:], cou[0, :].rearrange("(t p) -> p t", p=P))
+        scale_rows = x_scales[0].bitcast(I32)
+        for q in range(4):
+            nc.sync.dma_start(scale_table[:].bitcast(I32)[32 * q : 32 * q + 4, :], scale_rows[4 * q : 4 * q + 4, :])
+        nc.sync.dma_start(w_raw[:], w1.rearrange("(p j) n -> p j n", j=PACK))
+        nc.sync.dma_start(word_table[:].bitcast(I32), x_words[0].rearrange("p n t -> p (n t)").bitcast(I32))
+        nc.sync.dma_start(flow_sb[:], flow)
+        nc.sync.dma_start(infl_sb[:], infl)
+        nc.sync.dma_start(tra_sb[:], tra)
+        nc.sync.dma_start(trb_sb[:], trb)
+        nc.sync.dma_start(bank_sb[:], bank)
+
+        ident = sb.tile([P, P], F32, name="ident")
+        make_identity(nc, ident[:])
+
+        y_ps = [ps.tile([P, S], F32, name=f"y_ps{t}") for t in range(CHUNKS)]
+        a_ps = ps.tile([P, S], F32, name="a_ps")
+        rc_ps = ps.tile([P, S], F32, name="rc_ps")
+
+        den = sb.tile([P, 2 * CHUNKS], F32, name="den", tag="first_words", align_bytes=64)
+        rec = sb.tile([P, 2 * CHUNKS], F32, name="rec")
+        a_col = sb.tile([P, CHUNKS], F32, name="a_col")
+        nc.scalar.activation(den[:, :CHUNKS], c_col[:], ACT.Copy, bias=GUARD)
+        nc.scalar.activation(den[:, CHUNKS:], c_col[:], ACT.Copy, scale=1.5, bias=1.0)
+        nc.vector.reciprocal(rec[:], den[:])
+        nc.gpsimd.tensor_tensor(a_col[:], den[:, :CHUNKS], rec[:, CHUNKS:], ALU.mult)
+
+        for t in range(CHUNKS):
+            nc.tensor.transpose(rc_ps[:, chunk(t)], rec[:, t : t + 1].to_broadcast([P, P]), ident[:])
+
+        w_bf = sb.tile([P, N, PACK], BF16, name="w_bf", align_bytes=64)
+        nc.scalar.activation(w_bf[:], w_raw[:].rearrange("p j n -> p n j"), ACT.Copy)
+
+        x_sc = sb.tile([P, S], U8, name="x_sc", align_bytes=64)
+        nc.vector.tensor_copy(x_sc[:], scale_table[:].indirect(offs_sb[:]))
+
+        w_codes = sb.tile([P, N], U32, name="w_codes", align_bytes=64)
+        w_sc = sb.tile([P, N], U8, name="w_sc", align_bytes=64)
+        nc.vector.quantize_mx(out=w_codes[:].bitcast(FP8X4), scales=w_sc[:], in_=w_bf[:].rearrange("p n j -> p (n j)"))
+
+        x_codes = [sb.tile([P, P], U32, name=f"x_codes{t}", tag=("first_words" if t == 0 else f"words{t}"), align_bytes=64) for t in range(CHUNKS)]
+        mag = sb.tile([P, S], F32, name="mag")
+        decay = sb.tile([P, S], F32, name="decay")
+        for t in range(CHUNKS):
+            cols = chunk(t)
+            nc.vector.tensor_copy(x_codes[t][:], word_table[:].indirect(offs_sb[:, entries(cols)]))
+            nc.tensor.matmul_mx(out=y_ps[t][:, :P], lhsT=w_codes[:].bitcast(FP8X4), lhsT_scale=w_sc[:],
+                                rhs=x_codes[t][:].bitcast(FP8X4), rhs_scale=x_sc[:, cols], start=True, stop=True)
+            nc.scalar.activation(mag[:, cols], y_ps[t][:, :P], ACT.Abs)
+            nc.scalar.activation(decay[:, cols], mag[:, cols], ACT.Exp, scale=-1.0)
+
+        for t in range(CHUNKS):
+            nc.tensor.transpose(a_ps[:, chunk(t)], a_col[:, t : t + 1].to_broadcast([P, P]), ident[:])
+
+        def soft(h):
+            return mag[:, half(1 - h)]
+
+        for h in range(2):
+            nc.scalar.activation(soft(h), decay[:, half(h)], ACT.Ln, bias=1.0)
+
+        fk = sb.tile([P, S], F32, name="fk")
+        old = sb.tile([P, S], F32, name="old")
+        base = sb.tile([P, S], F32, name="base")
+        nc.vector.scalar_tensor_tensor(fk[:], rc_ps[:], -0.5, flow_sb[:], ALU.add, ALU.mult)
+        nc.vector.tensor_tensor(old[:], fk[:], infl_sb[:], ALU.add)
+        for t in range(CHUNKS):
+            nc.vector.scalar_tensor_tensor(base[:, chunk(t)], y_ps[t][:, :P], 0.0, old[:, chunk(t)], ALU.max, ALU.add)
+
+        ln_scale = sb.tile([P, CHUNKS], F32, name="ln_scale")
+        nbank = sb.tile([P, 1], F32, name="nbank")
+        nc.gpsimd.tensor_scalar(ln_scale[:], a_col[:], 2.3, 0.0, ALU.mult, ALU.add)
+        nc.gpsimd.tensor_scalar(nbank[:], bank_sb[:], -1.0 / SIGMA, 0.0, ALU.mult, ALU.add)
+
+        total = sb.tile([P, S], F32, name="total")
+        oa = sb.tile([P, S], F32, name="oa")
+        for h in range(2):
+            nc.vector.tensor_tensor(total[:, half(h)], soft(h), base[:, half(h)], ALU.add)
+        for h in range(2):
+            nc.vector.scalar_tensor_tensor(oa[:, half(h)], a_ps[:, half(h)], SIGMA, total[:, half(h)], ALU.mult, ALU.mult)
+
+        less_old = decay
+        less_oa = sb.tile([P, S], F32, name="less_oa")
+        nc.scalar.activation(less_old[:], old[:], ACT.Copy, scale=-1.3 / 2.3)
+        nc.scalar.activation(less_oa[:], oa[:], ACT.Copy, scale=-2.0 / 0.6)
+
+        ga = sb.tile([P, S], F32, name="ga")
+        gb = sb.tile([P, S], F32, name="gb")
+        for h in range(2):
+            nc.vector.tensor_copy(ga[:, half(h)], oa[:].indirect(tra_sb[:, entries(half(h))]))
+        for cols in (half(0), chunk(2), chunk(3)):
+            nc.vector.tensor_copy(gb[:, cols], oa[:].indirect(trb_sb[:, entries(cols)]))
+
+        terms = (total, less_old, less_oa, ga, gb)
+        for i, term in enumerate(terms):
+            for t in range(CHUNKS):
+                nc.tensor.matmul(y_ps[t][:, :P], lhsT=term[:, chunk(t)], rhs=ident[:], is_transpose=True,
+                                 start=(i == 0), stop=(i == len(terms) - 1))
+        logs = sb.tile([P, S], F32, name="logs")
+        for t in range(CHUNKS):
+            nc.scalar.activation(logs[:, chunk(t)], y_ps[t][:, :P], ACT.Ln, scale=ln_scale[:, t : t + 1], bias=0.1)
+
+        back = (y_ps[3], y_ps[2])
+        for t in range(CHUNKS):
+            nc.tensor.transpose(back[t // 2][:, chunk(t % 2)], logs[:, chunk(t)], ident[:])
+
+        stage = sb.tile([P, S], F32, name="stage")
+        res = sb.tile([P, S], F32, name="res")
+        for h in range(2):
+            nc.scalar.activation(stage[:, half(h)], back[h][:, :HALF], ACT.Exp, scale=0.6)
+            nc.vector.scalar_tensor_tensor(res[:, half(h)], oa[:, half(h)], nbank[:, 0:1], stage[:, half(h)], ALU.mult, ALU.add)
+            nc.sync.dma_start(out[:, half(h)], res[:, half(h)])

@@ -37,6 +37,12 @@ def tile_picked_ymuskr_stage_p_kernel(tc, x_words, x_scales, w1, flow, infl, cou
         def half(h):
             return slice(h * HALF, (h + 1) * HALF)
 
+        def dealt(ap):
+            return ap.rearrange("p (t q) -> p q t", t=PACK)
+
+        def plain(ap):
+            return ap.rearrange("p (q t) -> p q t", t=PACK)
+
         def entries(cols):
             return slice(cols.start // 16, cols.stop // 16)
 
@@ -44,8 +50,8 @@ def tile_picked_ymuskr_stage_p_kernel(tc, x_words, x_scales, w1, flow, infl, cou
         tra_sb = lists.tile([P, S // 16], U16, name="tra_sb")
         trb_sb = lists.tile([P, S // 16], U16, name="trb_sb")
 
-        scale_table = sb.tile([P, T], U8, name="scale_table", align_bytes=64)
-        word_table = sb.tile([P, T], U32, name="word_table", align_bytes=64)
+        scale_table = sb.tile([P, T], U8, name="scale_table", tag="scales_then_codes", align_bytes=64)
+        word_table = sb.tile([P, T], U32, name="word_table", tag="words_then_flow", align_bytes=64)
         w_raw = sb.tile([P, PACK, N], F32, name="w_raw")
         c_col = sb.tile([P, CHUNKS], F32, name="c_col")
         flow_sb = sb.tile([P, S], F32, name="flow_sb")
@@ -53,9 +59,8 @@ def tile_picked_ymuskr_stage_p_kernel(tc, x_words, x_scales, w1, flow, infl, cou
         bank_sb = sb.tile([P, 1], F32, name="bank_sb")
 
         nc.vector.memset(scale_table[:].bitcast(I32), 0)
+        nc.sync.dma_start(c_col[:], cou[0, :].rearrange("(p t) -> p t", p=P))
         nc.sync.dma_start(offs_sb[:], offs)
-        with nc.allow_non_contiguous_dma(reason="one routing number a partition and chunk"):
-            nc.sync.dma_start(c_col[:], cou[0, :].rearrange("(t p) -> p t", p=P))
         scale_rows = x_scales[0].bitcast(I32)
         for q in range(4):
             nc.sync.dma_start(scale_table[:].bitcast(I32)[32 * q : 32 * q + 4, :], scale_rows[4 * q : 4 * q + 4, :])
@@ -74,40 +79,41 @@ def tile_picked_ymuskr_stage_p_kernel(tc, x_words, x_scales, w1, flow, infl, cou
         a_ps = ps.tile([P, S], F32, name="a_ps")
         rc_ps = ps.tile([P, S], F32, name="rc_ps")
 
-        den = sb.tile([P, 2 * CHUNKS], F32, name="den", tag="first_words", align_bytes=64)
-        rec = sb.tile([P, 2 * CHUNKS], F32, name="rec")
-        a_col = sb.tile([P, CHUNKS], F32, name="a_col")
-        nc.scalar.activation(den[:, :CHUNKS], c_col[:], ACT.Copy, bias=GUARD)
-        nc.scalar.activation(den[:, CHUNKS:], c_col[:], ACT.Copy, scale=1.5, bias=1.0)
+        den = sb.tile([P, 2 * CHUNKS], F32, name="den", tag="den_then_bytes", align_bytes=64)
+        rec = sb.tile([P, 2 * CHUNKS], F32, name="rec", tag="rec_then_bytes", align_bytes=64)
+        a_col = sb.tile([P, CHUNKS], F32, name="a_col", tag="a_then_codes", align_bytes=64)
+        nc.vector.tensor_scalar(den[:, :CHUNKS], c_col[:], 1.0, GUARD, ALU.mult, ALU.add)
+        nc.vector.tensor_scalar(den[:, CHUNKS:], c_col[:], 1.5, 1.0, ALU.mult, ALU.add)
         nc.vector.reciprocal(rec[:], den[:])
-        nc.gpsimd.tensor_tensor(a_col[:], den[:, :CHUNKS], rec[:, CHUNKS:], ALU.mult)
+        c_safe = sb.tile([P, CHUNKS], F32, name="c_safe")
+        nc.gpsimd.tensor_scalar(c_safe[:], c_col[:], 1.0, GUARD, ALU.mult, ALU.add)
+        nc.gpsimd.tensor_tensor(a_col[:], c_safe[:], rec[:, CHUNKS:], ALU.mult)
 
         for t in range(CHUNKS):
             nc.tensor.transpose(rc_ps[:, chunk(t)], rec[:, t : t + 1].to_broadcast([P, P]), ident[:])
+        for t in range(CHUNKS):
+            nc.tensor.transpose(a_ps[:, chunk(t)], a_col[:, t : t + 1].to_broadcast([P, P]), ident[:])
 
-        w_bf = sb.tile([P, N, PACK], BF16, name="w_bf", align_bytes=64)
+        w_bf = sb.tile([P, N, PACK], BF16, name="w_bf", tag="staging", align_bytes=64)
         nc.scalar.activation(w_bf[:], w_raw[:].rearrange("p j n -> p n j"), ACT.Copy)
 
-        x_sc = sb.tile([P, S], U8, name="x_sc", align_bytes=64)
+        x_sc = sb.tile([P, S], U8, name="x_sc", tag="den_then_bytes", align_bytes=64)
         nc.vector.tensor_copy(x_sc[:], scale_table[:].indirect(offs_sb[:]))
 
-        w_codes = sb.tile([P, N], U32, name="w_codes", align_bytes=64)
-        w_sc = sb.tile([P, N], U8, name="w_sc", align_bytes=64)
+        w_codes = sb.tile([P, N], U32, name="w_codes", tag="a_then_codes", align_bytes=64)
+        w_sc = sb.tile([P, N], U8, name="w_sc", tag="rec_then_bytes", align_bytes=64)
         nc.vector.quantize_mx(out=w_codes[:].bitcast(FP8X4), scales=w_sc[:], in_=w_bf[:].rearrange("p n j -> p (n j)"))
 
-        x_codes = [sb.tile([P, P], U32, name=f"x_codes{t}", tag=("first_words" if t == 0 else f"words{t}"), align_bytes=64) for t in range(CHUNKS)]
         mag = sb.tile([P, S], F32, name="mag")
         decay = sb.tile([P, S], F32, name="decay")
         for t in range(CHUNKS):
             cols = chunk(t)
-            nc.vector.tensor_copy(x_codes[t][:], word_table[:].indirect(offs_sb[:, entries(cols)]))
+            x_codes = sb.tile([P, P], U32, name=f"x_codes{t}", tag=("staging", "scales_then_codes")[t % 2], align_bytes=64)
+            nc.vector.tensor_copy(x_codes[:], word_table[:].indirect(offs_sb[:, entries(cols)]))
             nc.tensor.matmul_mx(out=y_ps[t][:, :P], lhsT=w_codes[:].bitcast(FP8X4), lhsT_scale=w_sc[:],
-                                rhs=x_codes[t][:].bitcast(FP8X4), rhs_scale=x_sc[:, cols], start=True, stop=True)
+                                rhs=x_codes[:].bitcast(FP8X4), rhs_scale=x_sc[:, cols], start=True, stop=True)
             nc.scalar.activation(mag[:, cols], y_ps[t][:, :P], ACT.Abs)
             nc.scalar.activation(decay[:, cols], mag[:, cols], ACT.Exp, scale=-1.0)
-
-        for t in range(CHUNKS):
-            nc.tensor.transpose(a_ps[:, chunk(t)], a_col[:, t : t + 1].to_broadcast([P, P]), ident[:])
 
         def soft(h):
             return mag[:, half(1 - h)]
@@ -115,17 +121,16 @@ def tile_picked_ymuskr_stage_p_kernel(tc, x_words, x_scales, w1, flow, infl, cou
         for h in range(2):
             nc.scalar.activation(soft(h), decay[:, half(h)], ACT.Ln, bias=1.0)
 
-        fk = sb.tile([P, S], F32, name="fk")
+        fk = sb.tile([P, S], F32, name="fk", tag="words_then_flow", align_bytes=64)
         old = sb.tile([P, S], F32, name="old")
         base = sb.tile([P, S], F32, name="base")
-        nc.vector.scalar_tensor_tensor(fk[:], rc_ps[:], -0.5, flow_sb[:], ALU.add, ALU.mult)
+        nc.vector.scalar_tensor_tensor(plain(fk[:]), dealt(rc_ps[:]), -0.5, plain(flow_sb[:]), ALU.add, ALU.mult)
         nc.vector.tensor_tensor(old[:], fk[:], infl_sb[:], ALU.add)
         for t in range(CHUNKS):
             nc.vector.scalar_tensor_tensor(base[:, chunk(t)], y_ps[t][:, :P], 0.0, old[:, chunk(t)], ALU.max, ALU.add)
 
         ln_scale = sb.tile([P, CHUNKS], F32, name="ln_scale")
         nbank = sb.tile([P, 1], F32, name="nbank")
-        nc.gpsimd.tensor_scalar(ln_scale[:], a_col[:], 2.3, 0.0, ALU.mult, ALU.add)
         nc.gpsimd.tensor_scalar(nbank[:], bank_sb[:], -1.0 / SIGMA, 0.0, ALU.mult, ALU.add)
 
         total = sb.tile([P, S], F32, name="total")
@@ -133,12 +138,17 @@ def tile_picked_ymuskr_stage_p_kernel(tc, x_words, x_scales, w1, flow, infl, cou
         for h in range(2):
             nc.vector.tensor_tensor(total[:, half(h)], soft(h), base[:, half(h)], ALU.add)
         for h in range(2):
-            nc.vector.scalar_tensor_tensor(oa[:, half(h)], a_ps[:, half(h)], SIGMA, total[:, half(h)], ALU.mult, ALU.mult)
+            nc.vector.scalar_tensor_tensor(plain(oa[:, half(h)]), dealt(a_ps[:])[:, 64 * h : 64 * (h + 1), :], SIGMA, plain(total[:, half(h)]), ALU.mult, ALU.mult)
 
         less_old = decay
         less_oa = sb.tile([P, S], F32, name="less_oa")
         nc.scalar.activation(less_old[:], old[:], ACT.Copy, scale=-1.3 / 2.3)
+        a_rows = mag
+        nc.scalar.activation(plain(a_rows[:]), dealt(a_ps[:]), ACT.Copy, scale=2.3)
         nc.scalar.activation(less_oa[:], oa[:], ACT.Copy, scale=-2.0 / 0.6)
+        for t in range(CHUNKS):
+            nc.tensor.transpose(rc_ps[:, chunk(t)], a_rows[:, chunk(t)], ident[:])
+        nc.scalar.activation(ln_scale[:], rc_ps[:].rearrange("p (t m) -> p t m", t=CHUNKS)[:, :, 0], ACT.Copy)
 
         ga = sb.tile([P, S], F32, name="ga")
         gb = sb.tile([P, S], F32, name="gb")

@@ -37,12 +37,6 @@ def tile_picked_ymuskr_stage_p_kernel(tc, x_words, x_scales, w1, flow, infl, cou
         def half(h):
             return slice(h * HALF, (h + 1) * HALF)
 
-        def dealt(ap):
-            return ap.rearrange("p (t q) -> p q t", t=PACK)
-
-        def plain(ap):
-            return ap.rearrange("p (q t) -> p q t", t=PACK)
-
         def entries(cols):
             return slice(cols.start // 16, cols.stop // 16)
 
@@ -50,17 +44,18 @@ def tile_picked_ymuskr_stage_p_kernel(tc, x_words, x_scales, w1, flow, infl, cou
         tra_sb = lists.tile([P, S // 16], U16, name="tra_sb")
         trb_sb = lists.tile([P, S // 16], U16, name="trb_sb")
 
-        scale_table = sb.tile([P, T], U8, name="scale_table", tag="scales_then_codes", align_bytes=64)
+        scale_table = sb.tile([P, T], U8, name="scale_table", align_bytes=64)
         word_table = sb.tile([P, T], U32, name="word_table", tag="words_then_flow", align_bytes=64)
-        w_raw = sb.tile([P, PACK, N], F32, name="w_raw")
+        w_raw = sb.tile([P, PACK, N], F32, name="w_raw", tag="raw_then_bytes", align_bytes=64)
         c_col = sb.tile([P, CHUNKS], F32, name="c_col")
         flow_sb = sb.tile([P, S], F32, name="flow_sb")
         infl_sb = sb.tile([P, S], F32, name="infl_sb")
         bank_sb = sb.tile([P, 1], F32, name="bank_sb")
 
         nc.vector.memset(scale_table[:].bitcast(I32), 0)
-        nc.sync.dma_start(c_col[:], cou[0, :].rearrange("(p t) -> p t", p=P))
         nc.sync.dma_start(offs_sb[:], offs)
+        with nc.allow_non_contiguous_dma(reason="one routing number a partition and chunk"):
+            nc.sync.dma_start(c_col[:], cou[0, :].rearrange("(t p) -> p t", p=P))
         scale_rows = x_scales[0].bitcast(I32)
         for q in range(4):
             nc.sync.dma_start(scale_table[:].bitcast(I32)[32 * q : 32 * q + 4, :], scale_rows[4 * q : 4 * q + 4, :])
@@ -88,6 +83,8 @@ def tile_picked_ymuskr_stage_p_kernel(tc, x_words, x_scales, w1, flow, infl, cou
         c_safe = sb.tile([P, CHUNKS], F32, name="c_safe")
         nc.gpsimd.tensor_scalar(c_safe[:], c_col[:], 1.0, GUARD, ALU.mult, ALU.add)
         nc.gpsimd.tensor_tensor(a_col[:], c_safe[:], rec[:, CHUNKS:], ALU.mult)
+        ln_scale = sb.tile([P, CHUNKS], F32, name="ln_scale")
+        nc.gpsimd.tensor_scalar(ln_scale[:], a_col[:], 2.3, 0.0, ALU.mult, ALU.add)
 
         for t in range(CHUNKS):
             nc.tensor.transpose(rc_ps[:, chunk(t)], rec[:, t : t + 1].to_broadcast([P, P]), ident[:])
@@ -106,13 +103,13 @@ def tile_picked_ymuskr_stage_p_kernel(tc, x_words, x_scales, w1, flow, infl, cou
 
         mag = sb.tile([P, S], F32, name="mag")
         decay = sb.tile([P, S], F32, name="decay")
-        for t in range(CHUNKS):
-            cols = chunk(t)
-            x_codes = sb.tile([P, P], U32, name=f"x_codes{t}", tag=("staging", "scales_then_codes")[t % 2], align_bytes=64)
+        for h in range(2):
+            cols = half(h)
+            x_codes = sb.tile([P, HALF], U32, name=f"x_codes{h}", tag=("staging", "raw_then_bytes")[h], align_bytes=64)
             nc.vector.tensor_copy(x_codes[:], word_table[:].indirect(offs_sb[:, entries(cols)]))
-            nc.tensor.matmul_mx(out=y_ps[t][:, :P], lhsT=w_codes[:].bitcast(FP8X4), lhsT_scale=w_sc[:],
+            nc.tensor.matmul_mx(out=y_ps[h][:, :HALF], lhsT=w_codes[:].bitcast(FP8X4), lhsT_scale=w_sc[:],
                                 rhs=x_codes[:].bitcast(FP8X4), rhs_scale=x_sc[:, cols], start=True, stop=True)
-            nc.scalar.activation(mag[:, cols], y_ps[t][:, :P], ACT.Abs)
+            nc.scalar.activation(mag[:, cols], y_ps[h][:, :HALF], ACT.Abs)
             nc.scalar.activation(decay[:, cols], mag[:, cols], ACT.Exp, scale=-1.0)
 
         def soft(h):
@@ -124,13 +121,14 @@ def tile_picked_ymuskr_stage_p_kernel(tc, x_words, x_scales, w1, flow, infl, cou
         fk = sb.tile([P, S], F32, name="fk", tag="words_then_flow", align_bytes=64)
         old = sb.tile([P, S], F32, name="old")
         base = sb.tile([P, S], F32, name="base")
-        nc.vector.scalar_tensor_tensor(plain(fk[:]), dealt(rc_ps[:]), -0.5, plain(flow_sb[:]), ALU.add, ALU.mult)
+        nc.vector.scalar_tensor_tensor(fk[:], rc_ps[:], -0.5, flow_sb[:], ALU.add, ALU.mult)
         nc.vector.tensor_tensor(old[:], fk[:], infl_sb[:], ALU.add)
-        for t in range(CHUNKS):
-            nc.vector.scalar_tensor_tensor(base[:, chunk(t)], y_ps[t][:, :P], 0.0, old[:, chunk(t)], ALU.max, ALU.add)
+        for h in range(2):
+            nc.vector.scalar_tensor_tensor(base[:, half(h)], y_ps[h][:, :HALF], 0.0, old[:, half(h)], ALU.max, ALU.add)
 
-        ln_scale = sb.tile([P, CHUNKS], F32, name="ln_scale")
         nbank = sb.tile([P, 1], F32, name="nbank")
+        less_old = sb.tile([P, S], F32, name="less_old")
+        nc.vector.tensor_scalar(less_old[:], old[:], -1.3 / 2.3, None, ALU.mult)
         nc.gpsimd.tensor_scalar(nbank[:], bank_sb[:], -1.0 / SIGMA, 0.0, ALU.mult, ALU.add)
 
         total = sb.tile([P, S], F32, name="total")
@@ -138,17 +136,10 @@ def tile_picked_ymuskr_stage_p_kernel(tc, x_words, x_scales, w1, flow, infl, cou
         for h in range(2):
             nc.vector.tensor_tensor(total[:, half(h)], soft(h), base[:, half(h)], ALU.add)
         for h in range(2):
-            nc.vector.scalar_tensor_tensor(plain(oa[:, half(h)]), dealt(a_ps[:])[:, 64 * h : 64 * (h + 1), :], SIGMA, plain(total[:, half(h)]), ALU.mult, ALU.mult)
+            nc.vector.scalar_tensor_tensor(oa[:, half(h)], a_ps[:, half(h)], SIGMA, total[:, half(h)], ALU.mult, ALU.mult)
 
-        less_old = decay
         less_oa = sb.tile([P, S], F32, name="less_oa")
-        nc.scalar.activation(less_old[:], old[:], ACT.Copy, scale=-1.3 / 2.3)
-        a_rows = mag
-        nc.scalar.activation(plain(a_rows[:]), dealt(a_ps[:]), ACT.Copy, scale=2.3)
         nc.scalar.activation(less_oa[:], oa[:], ACT.Copy, scale=-2.0 / 0.6)
-        for t in range(CHUNKS):
-            nc.tensor.transpose(rc_ps[:, chunk(t)], a_rows[:, chunk(t)], ident[:])
-        nc.scalar.activation(ln_scale[:], rc_ps[:].rearrange("p (t m) -> p t m", t=CHUNKS)[:, :, 0], ACT.Copy)
 
         ga = sb.tile([P, S], F32, name="ga")
         gb = sb.tile([P, S], F32, name="gb")
@@ -157,7 +148,7 @@ def tile_picked_ymuskr_stage_p_kernel(tc, x_words, x_scales, w1, flow, infl, cou
         for cols in (half(0), chunk(2), chunk(3)):
             nc.vector.tensor_copy(gb[:, cols], oa[:].indirect(trb_sb[:, entries(cols)]))
 
-        terms = (total, less_old, less_oa, ga, gb)
+        terms = (less_old, total, less_oa, ga, gb)
         for i, term in enumerate(terms):
             for t in range(CHUNKS):
                 nc.tensor.matmul(y_ps[t][:, :P], lhsT=term[:, chunk(t)], rhs=ident[:], is_transpose=True,

from contextlib import ExitStack

import concourse.mybir as mybir
from concourse.masks import make_identity

K, T, S, N = 512, 1024, 512, 128
FLOPS = 2 * K * N * S

F32 = mybir.dt.float32
BF16 = mybir.dt.bfloat16
I32 = mybir.dt.int32
U32 = mybir.dt.uint32
U16 = mybir.dt.uint16
U8 = mybir.dt.uint8
FP8X4 = mybir.dt.float8_e4m3fn_x4
ALU = mybir.AluOpType
ACT = mybir.ActivationFunctionType

P = 128
PACK = 4
CHUNKS = S // P
HALF = S // 2
SIGMA = 0.6 / 2.3
GUARD = 2.0 ** -40


def tile_picked_ymuskr_stage_p_kernel(tc, x_words, x_scales, w1, flow, infl, cou, bank, offs, tra, trb, out):
    nc = tc.nc
    with ExitStack() as ctx:
        lists = ctx.enter_context(tc.tile_pool(name="lists", bufs=1))
        sb = ctx.enter_context(tc.tile_pool(name="sb", bufs=1))
        ps = ctx.enter_context(tc.psum_pool(name="ps", bufs=1))

        def chunk(t):
            return slice(t * P, (t + 1) * P)

        def half(h):
            return slice(h * HALF, (h + 1) * HALF)

        def entries(cols):
            return slice(cols.start // 16, cols.stop // 16)

        offs_sb = lists.tile([P, S // 16], U16, name="offs_sb")
        tra_sb = lists.tile([P, S // 16], U16, name="tra_sb")
        trb_sb = lists.tile([P, S // 16], U16, name="trb_sb")

        scale_table = sb.tile([P, T], U8, name="scale_table", align_bytes=64)
        word_table = sb.tile([P, T], U32, name="word_table", tag="words_then_flow", align_bytes=64)
        w_raw = sb.tile([P, PACK, N], F32, name="w_raw", tag="raw_then_bytes", align_bytes=64)
        c_col = sb.tile([P, CHUNKS], F32, name="c_col")
        flow_sb = sb.tile([P, S], F32, name="flow_sb")
        infl_sb = sb.tile([P, S], F32, name="infl_sb")
        bank_sb = sb.tile([P, 1], F32, name="bank_sb")

        nc.vector.memset(scale_table[:].bitcast(I32), 0)
        nc.sync.dma_start(offs_sb[:], offs)
        with nc.allow_non_contiguous_dma(reason="one routing number a partition and chunk"):
            nc.sync.dma_start(c_col[:], cou[0, :].rearrange("(t p) -> p t", p=P))
        scale_rows = x_scales[0].bitcast(I32)
        for q in range(4):
            nc.sync.dma_start(scale_table[:].bitcast(I32)[32 * q : 32 * q + 4, :], scale_rows[4 * q : 4 * q + 4, :])
        nc.sync.dma_start(w_raw[:], w1.rearrange("(p j) n -> p j n", j=PACK))
        nc.sync.dma_start(word_table[:].bitcast(I32), x_words[0].rearrange("p n t -> p (n t)").bitcast(I32))
        nc.sync.dma_start(flow_sb[:], flow)
        nc.sync.dma_start(infl_sb[:], infl)
        nc.sync.dma_start(tra_sb[:], tra)
        nc.sync.dma_start(trb_sb[:], trb)
        nc.sync.dma_start(bank_sb[:], bank)

        ident = sb.tile([P, P], F32, name="ident")
        make_identity(nc, ident[:])

        y_ps = [ps.tile([P, S], F32, name=f"y_ps{t}") for t in range(CHUNKS)]
        a_ps = ps.tile([P, S], F32, name="a_ps")
        rc_ps = ps.tile([P, S], F32, name="rc_ps")

        den = sb.tile([P, 2 * CHUNKS], F32, name="den", tag="den_then_bytes", align_bytes=64)
        rec = sb.tile([P, 2 * CHUNKS], F32, name="rec", tag="rec_then_bytes", align_bytes=64)
        a_col = sb.tile([P, CHUNKS], F32, name="a_col", tag="a_then_codes", align_bytes=64)
        nc.vector.tensor_scalar(den[:, :CHUNKS], c_col[:], 1.0, GUARD, ALU.mult, ALU.add)
        nc.vector.tensor_scalar(den[:, CHUNKS:], c_col[:], 1.5, 1.0, ALU.mult, ALU.add)
        nc.vector.reciprocal(rec[:], den[:])
        c_safe = sb.tile([P, CHUNKS], F32, name="c_safe")
        nc.gpsimd.tensor_scalar(c_safe[:], c_col[:], 1.0, GUARD, ALU.mult, ALU.add)
        nc.gpsimd.tensor_tensor(a_col[:], c_safe[:], rec[:, CHUNKS:], ALU.mult)
        ln_scale = sb.tile([P, CHUNKS], F32, name="ln_scale")
        nc.gpsimd.tensor_scalar(ln_scale[:], a_col[:], 2.3, 0.0, ALU.mult, ALU.add)

        for t in range(CHUNKS):
            nc.tensor.transpose(rc_ps[:, chunk(t)], rec[:, t : t + 1].to_broadcast([P, P]), ident[:])
        for t in range(CHUNKS):
            nc.tensor.transpose(a_ps[:, chunk(t)], a_col[:, t : t + 1].to_broadcast([P, P]), ident[:])

        w_bf = sb.tile([P, N, PACK], BF16, name="w_bf", tag="staging", align_bytes=64)
        nc.scalar.activation(w_bf[:], w_raw[:].rearrange("p j n -> p n j"), ACT.Copy)

        x_sc = sb.tile([P, S], U8, name="x_sc", tag="den_then_bytes", align_bytes=64)
        nc.vector.tensor_copy(x_sc[:], scale_table[:].indirect(offs_sb[:]))

        w_codes = sb.tile([P, N], U32, name="w_codes", tag="a_then_codes", align_bytes=64)
        w_sc = sb.tile([P, N], U8, name="w_sc", tag="rec_then_bytes", align_bytes=64)
        nc.vector.quantize_mx(out=w_codes[:].bitcast(FP8X4), scales=w_sc[:], in_=w_bf[:].rearrange("p n j -> p (n j)"))

        mag = sb.tile([P, S], F32, name="mag")
        decay = sb.tile([P, S], F32, name="decay")
        for h in range(2):
            cols = half(h)
            x_codes = sb.tile([P, HALF], U32, name=f"x_codes{h}", tag=("staging", "raw_then_bytes")[h], align_bytes=64)
            nc.vector.tensor_copy(x_codes[:], word_table[:].indirect(offs_sb[:, entries(cols)]))
            nc.tensor.matmul_mx(out=y_ps[h][:, :HALF], lhsT=w_codes[:].bitcast(FP8X4), lhsT_scale=w_sc[:],
                                rhs=x_codes[:].bitcast(FP8X4), rhs_scale=x_sc[:, cols], start=True, stop=True)
            nc.scalar.activation(mag[:, cols], y_ps[h][:, :HALF], ACT.Abs)
            nc.scalar.activation(decay[:, cols], mag[:, cols], ACT.Exp, scale=-1.0)

        def soft(h):
            return mag[:, half(1 - h)]

        for h in range(2):
            nc.scalar.activation(soft(h), decay[:, half(h)], ACT.Ln, bias=1.0)

        fk = sb.tile([P, S], F32, name="fk", tag="words_then_flow", align_bytes=64)
        old = sb.tile([P, S], F32, name="old")
        base = sb.tile([P, S], F32, name="base")
        nc.vector.scalar_tensor_tensor(fk[:], rc_ps[:], -0.5, flow_sb[:], ALU.add, ALU.mult)
        nc.vector.tensor_tensor(old[:], fk[:], infl_sb[:], ALU.add)
        for h in range(2):
            nc.vector.scalar_tensor_tensor(base[:, half(h)], y_ps[h][:, :HALF], 0.0, old[:, half(h)], ALU.max, ALU.add)

        nbank = sb.tile([P, 1], F32, name="nbank")
        less_old = sb.tile([P, S], F32, name="less_old")
        nc.vector.tensor_scalar(less_old[:], old[:], -1.3 / 2.3, None, ALU.mult)
        nc.gpsimd.tensor_scalar(nbank[:], bank_sb[:], -1.0 / SIGMA, 0.0, ALU.mult, ALU.add)

        total = sb.tile([P, S], F32, name="total")
        oa = sb.tile([P, S], F32, name="oa")
        for h in range(2):
            nc.vector.tensor_tensor(total[:, half(h)], soft(h), base[:, half(h)], ALU.add)
        for h in range(2):
            nc.vector.scalar_tensor_tensor(oa[:, half(h)], a_ps[:, half(h)], SIGMA, total[:, half(h)], ALU.mult, ALU.mult)

        less_oa = sb.tile([P, S], F32, name="less_oa")
        nc.scalar.activation(less_oa[:], oa[:], ACT.Copy, scale=-2.0 / 0.6)

        ga = sb.tile([P, S], F32, name="ga")
        gb = sb.tile([P, S], F32, name="gb")
        for h in range(2):
            nc.vector.tensor_copy(ga[:, half(h)], oa[:].indirect(tra_sb[:, entries(half(h))]))
        for cols in (half(0), chunk(2), chunk(3)):
            nc.vector.tensor_copy(gb[:, cols], oa[:].indirect(trb_sb[:, entries(cols)]))

        terms = (less_old, total, less_oa, ga, gb)
        for i, term in enumerate(terms):
            for t in range(CHUNKS):
                nc.tensor.matmul(y_ps[t][:, :P], lhsT=term[:, chunk(t)], rhs=ident[:], is_transpose=True,
                                 start=(i == 0), stop=(i == len(terms) - 1))
        logs = sb.tile([P, S], F32, name="logs")
        for t in range(CHUNKS):
            nc.scalar.activation(logs[:, chunk(t)], y_ps[t][:, :P], ACT.Ln, scale=ln_scale[:, t : t + 1], bias=0.1)

        back = (y_ps[3], y_ps[2])
        for t in range(CHUNKS):
            nc.tensor.transpose(back[t // 2][:, chunk(t % 2)], logs[:, chunk(t)], ident[:])

        stage = sb.tile([P, S], F32, name="stage")
        res = sb.tile([P, S], F32, name="res")
        for h in range(2):
            nc.scalar.activation(stage[:, half(h)], back[h][:, :HALF], ACT.Exp, scale=0.6)
            nc.vector.scalar_tensor_tensor(res[:, half(h)], oa[:, half(h)], nbank[:, 0:1], stage[:, half(h)], ALU.mult, ALU.add)
            nc.sync.dma_start(out[:, half(h)], res[:, half(h)])
